import numpy as np
import ml_dtypes


def mxq(x, axis, fmt="e4m3"):
    dtype, down = {"e4m3": (ml_dtypes.float8_e4m3fn, 7), "e5m2": (ml_dtypes.float8_e5m2, 14)}[fmt]
    v = np.moveaxis(np.asarray(x, np.float32).astype(ml_dtypes.bfloat16).astype(np.float64), axis, -1)
    blocks = v.reshape(v.shape[:-1] + (-1, 32))
    amax = np.abs(blocks).max(-1, keepdims=True)
    byte = np.maximum(np.where(amax > 0, np.frexp(amax)[1] - 1 + 127, 0) - down, 1)
    scale = np.exp2(byte - 127.0)
    codes = (blocks / scale).astype(np.float32).astype(dtype).astype(np.float64)
    return np.moveaxis((codes * scale).reshape(v.shape), -1, axis)


WIDE = False


def mx_kscale(k):
    if not WIDE:
        return np.ones(k)
    levels = np.array([10, -10, 5, -5, 0])
    if k % 512:
        return np.exp2(np.random.permutation(np.resize(levels, k // 32))).repeat(32)
    a = np.empty((k // 512, 16))
    for p in range(k // 512):
        a[p, :8] = np.random.permutation(np.resize(levels, 8))
        for g in range(8):
            far = levels[np.abs(levels - a[p, g]) >= 10]
            a[p, g + 8] = far[np.random.randint(len(far))]
    return np.exp2(a.ravel()).repeat(32)


def f64(x):
    return np.asarray(x).astype(np.float64)


def striped(idx):
    return np.tile(idx.reshape(-1, 16).T, (8, 1)).astype(np.uint16)


def unstriped(offs):
    return offs[:16].T.reshape(-1).astype(np.int64)


E2M1 = np.array([0.0, 0.5, 1.0, 1.5, 2.0, 3.0, 4.0, 6.0, -0.0, -0.5, -1.0, -1.5, -2.0, -3.0, -4.0, -6.0])


def pack_weight(w, fmt):
    k, n = w.shape
    w = f64(np.asarray(w, np.float32).astype(ml_dtypes.bfloat16)).reshape(k // 32, 32, n)
    amax = np.abs(w).max(1)
    if fmt == "e4m3":
        byte = np.frexp(amax)[1] - 1 + 127 - 7
    else:
        mant, ex = np.frexp(amax / 6.0)
        byte = np.where(mant > 0.5, ex, ex - 1) + 127
    byte = np.clip(np.where(amax > 0, byte, 1), 1, 254)
    scaled = (w * np.exp2(127.0 - byte)[:, None, :]).reshape(k, n).astype(np.float32)
    by_word = np.ascontiguousarray(scaled.reshape(k // 512, 128, 4, n).transpose(0, 1, 3, 2))
    if fmt == "e4m3":
        words = by_word.astype(ml_dtypes.float8_e4m3fn).view(np.uint8)
    else:
        c = by_word.astype(ml_dtypes.float4_e2m1fn).view(np.uint8) & 0xF
        words = (c[..., 0::2] | (c[..., 1::2] << 4)).reshape(k // 512, 128, 2 * n)
    return np.ascontiguousarray(words), np.ascontiguousarray(byte.astype(np.uint8).reshape(k // 512, 16, n))


def unpack_weight(words, scales, fmt):
    g, _, n = scales.shape
    words = np.ascontiguousarray(words).reshape(g, 128, n, -1)
    if fmt == "e4m3":
        vals = words.view(ml_dtypes.float8_e4m3fn).astype(np.float64)
    else:
        nib = np.empty((g, 128, n, 4), np.uint8)
        nib[..., 0::2] = words & 0xF
        nib[..., 1::2] = words >> 4
        vals = E2M1[nib]
    vals = vals * np.repeat(np.exp2(scales.astype(np.float64) - 127.0), 8, axis=1)[..., None]
    return vals.transpose(0, 1, 3, 2).reshape(g * 512, n)


def pack_table(v):
    words, scales = pack_weight(v, "e4m3")
    return np.concatenate([words.reshape(words.shape[0], -1), scales.reshape(scales.shape[0], -1)], axis=1)


def unpack_table(tab):
    g, t = tab.shape[0], tab.shape[1] // 528
    return unpack_weight(tab[:, :512 * t].reshape(g, 128, t, 4), tab[:, 512 * t:].reshape(g, 16, t), "e4m3")


K, M, T, S = 2048, 256, 512, 256


def setup_inputs():
    n = np.random.standard_normal
    s = mx_kscale(K)[:, None]
    s2 = mx_kscale(512)[:, None]
    p_w4 = pack_weight(n((K, M)) / np.sqrt(K) / s, "e2m1")
    return {
        "tab": pack_table(n((K, T)) * s),
        "w4_words": p_w4[0],
        "w4_scales": p_w4[1],
        "c": (n((512, S)) * s2).astype(np.float32),
        "u": (n((512, M)) / np.sqrt(512) / s2).astype(np.float32),
        "wgo": np.tile(np.random.uniform(0.5, 2.0, S), (128, 1)).astype(np.float32),
        "offs": striped(np.random.permutation(T)[:S]),
        "offs2": striped(np.random.permutation(T)[:S]),
    }


def reference(tab, w4_words, w4_scales, c, u, wgo, offs, offs2):
    tab_ = unpack_table(tab)[:, unstriped(offs)]
    w4_ = unpack_weight(w4_words, w4_scales, "e2m1")
    c_ = mxq(f64(c), 0, "e4m3")
    u_ = mxq(f64(u), 0, "e4m3")
    y = w4_.T @ tab_ + u_.T @ c_
    out = np.zeros((M, T))
    out[:, unstriped(offs2)] = f64(wgo)[0] * (y)
    return out

@@ -1,0 +1,168 @@
+from contextlib import ExitStack
+
+import concourse.mybir as mybir
+
+K, M, T, S, L = 2048, 256, 512, 256, 512
+FLOPS = 2 * (K + L) * M * S
+
+F32 = mybir.dt.float32
+BF16 = mybir.dt.bfloat16
+I32 = mybir.dt.int32
+U32 = mybir.dt.uint32
+U16 = mybir.dt.uint16
+U8 = mybir.dt.uint8
+FP8X4 = mybir.dt.float8_e4m3fn_x4
+FP4X4 = mybir.dt.float4_e2m1fn_x4
+MULT = mybir.AluOpType.mult
+
+P = 128
+PACK = 4
+PASSES = K // (P * PACK)
+HALF = 128
+LIST_COLS = HALF // 16
+
+
+def tile_list_tabscat_d_none_kernel(tc, tab, w4_words, w4_scales, c, u, wgo, offs, offs2, out):
+    nc = tc.nc
+    with ExitStack() as ctx:
+        keep = ctx.enter_context(tc.tile_pool(name="keep", bufs=1))
+        ring = ctx.enter_context(tc.tile_pool(name="ring", bufs=2))
+        psum = ctx.enter_context(tc.psum_pool(name="psum", bufs=2))
+
+        idx = keep.tile([P, S // 16], U16, name="idx")
+        idx2 = keep.tile([P, S // 16], U16, name="idx2")
+        win = keep.tile([P, T], U8, name="win", align_bytes=64)
+        w4 = keep.tile([P, PASSES, 2 * M], U8, name="w4", align_bytes=64)
+        rows = keep.tile([64, S + M], U8, name="rows", align_bytes=64)
+        planes = keep.tile([P, PASSES * (S + M)], U8, name="planes", align_bytes=64)
+        c_raw = keep.tile([P, PACK, S], F32, name="c_raw", tag="c_wgo", align_bytes=64)
+        u_raw = keep.tile([P, PACK, M], F32, name="u_raw", align_bytes=64)
+        pages = [keep.tile([P, T], F32, name="page%d" % m, align_bytes=64) for m in range(2)]
+
+        nc.vector.memset(win[64:128, :].bitcast(I32), 0)
+        for m in range(2):
+            nc.vector.memset(pages[m][:], 0.0)
+
+        def load_words(a):
+            words = ring.tile([P, T], U32, name="words", align_bytes=64)
+            nc.sync.dma_start(
+                out=words[:].bitcast(I32),
+                in_=tab[a, 0 : 4 * P * T].rearrange("(p x) -> p x", p=P).bitcast(I32),
+            )
+            return words
+
+        nc.sync.dma_start(idx[:], offs)
+        nc.sync.dma_start(
+            out=win[0:64, :].bitcast(I32),
+            in_=tab[:, 4 * P * T :].rearrange("a (q t) -> q a t", q=16).bitcast(I32),
+        )
+        nc.scalar.dma_start(out=rows[:, S:].bitcast(I32), in_=w4_scales.rearrange("a q n -> q a n").bitcast(I32))
+        words0 = load_words(0)
+        nc.sync.dma_start(idx2[:], offs2)
+        words1 = load_words(1)
+        nc.sync.dma_start(out=w4[:].bitcast(I32), in_=w4_words.rearrange("a p n -> p a n").bitcast(I32))
+        nc.sync.dma_start(out=c_raw[:], in_=c.rearrange("(p j) w -> p j w", j=PACK))
+        nc.sync.dma_start(out=u_raw[:], in_=u.rearrange("(p j) w -> p j w", j=PACK))
+
+        picked = [keep.tile([P, S], U32, name="picked%d" % a, align_bytes=64) for a in range(PASSES)]
+
+        def gather(a, words, lo, hi):
+            nc.vector.tensor_copy(
+                picked[a][:, lo * HALF : hi * HALF], words[:].indirect(idx[:, lo * LIST_COLS : hi * LIST_COLS])
+            )
+
+        picked_scales = keep.tile([P, S], U8, name="picked_scales", align_bytes=64)
+        nc.vector.tensor_copy(picked_scales[:], win[:].indirect(idx[:]))
+        nc.vector.tensor_copy(rows[:, :S].bitcast(I32), picked_scales[0:64, :].bitcast(I32))
+        for q in range(4):
+            nc.scalar.dma_start(
+                out=planes[32 * q : 32 * q + 4, :].rearrange("r (a n) -> r a n", a=PASSES).bitcast(I32),
+                in_=rows[16 * q : 16 * q + 16, :].bitcast(I32),
+            )
+        gather(0, words0, 0, 2)
+        words2 = load_words(2)
+        gather(1, words1, 0, 2)
+        words3 = load_words(3)
+
+        def views(raw, grouped):
+            return (
+                grouped.rearrange("p (c i t) -> p c t i", i=4, t=PACK),
+                raw.rearrange("p t (c i) -> p c t i", i=4),
+            )
+
+        c_bf = keep.tile([P, PACK * S], BF16, name="c_bf", align_bytes=64)
+        c_codes = keep.tile([P, S], U32, name="c_codes", align_bytes=64)
+        c_plane = keep.tile([P, S], U8, name="c_plane", align_bytes=64)
+        u_bf = [keep.tile([P, PACK * HALF], BF16, name="u_bf%d" % m, align_bytes=64) for m in range(2)]
+        u_codes = [keep.tile([P, HALF], U32, name="u_codes%d" % m, align_bytes=64) for m in range(2)]
+        u_plane = [keep.tile([P, HALF], U8, name="u_plane%d" % m, align_bytes=64) for m in range(2)]
+        acc = {}
+
+        def table_pass(a, m, h, start, stop):
+            at = a * (S + M)
+            nc.tensor.matmul_mx(
+                out=acc[m, h][:],
+                lhsT=w4[:, a, 2 * m * HALF : 2 * (m + 1) * HALF].bitcast(FP4X4),
+                lhsT_scale=planes[:, at + S + m * HALF : at + S + (m + 1) * HALF],
+                rhs=picked[a][:, h * HALF : (h + 1) * HALF].bitcast(FP8X4),
+                rhs_scale=planes[:, at + h * HALF : at + (h + 1) * HALF],
+                start=start,
+                stop=stop,
+            )
+
+        def dense_pass(m, h):
+            nc.tensor.matmul_mx(
+                out=acc[m, h][:],
+                lhsT=u_codes[m][:].bitcast(FP8X4),
+                lhsT_scale=u_plane[m][:],
+                rhs=c_codes[:, h * HALF : (h + 1) * HALF].bitcast(FP8X4),
+                rhs_scale=c_plane[:, h * HALF : (h + 1) * HALF],
+                start=False,
+                stop=False,
+            )
+
+        dst, src = views(c_raw[:], c_bf[:])
+        nc.vector.tensor_copy(out=dst, in_=src)
+        weight = keep.tile([P, S], F32, name="weight", tag="c_wgo", align_bytes=64)
+        nc.sync.dma_start(out=weight[:], in_=wgo)
+        dst, src = views(u_raw[:, :, HALF:], u_bf[1][:])
+        nc.scalar.copy(out=dst, in_=src)
+        nc.vector.quantize_mx(out=c_codes[:].bitcast(FP8X4), scales=c_plane[:], in_=c_bf[:])
+        dst, src = views(u_raw[:, :, :HALF], u_bf[0][:])
+        nc.vector.tensor_copy(out=dst, in_=src)
+        gather(2, words2, 0, 1)
+        nc.vector.quantize_mx(out=u_codes[0][:].bitcast(FP8X4), scales=u_plane[0][:], in_=u_bf[0][:])
+        gather(3, words3, 0, 1)
+
+        def finish(m, h):
+            acc.setdefault((m, h), psum.tile([P, HALF], F32, name="acc"))
+            table_pass(0, m, h, True, False)
+            table_pass(1, m, h, False, False)
+            dense_pass(m, h)
+            table_pass(2, m, h, False, False)
+            table_pass(3, m, h, False, True)
+            y = keep.tile([P, HALF], F32, name="y%d%d" % (m, h), align_bytes=64)
+            nc.scalar.copy(out=y[:], in_=acc[m, h][:])
+            return y
+
+        def place(m, h, y):
+            nc.vector.tensor_tensor(
+                pages[m][:].indirect(idx2[:, h * LIST_COLS : (h + 1) * LIST_COLS]),
+                y[:],
+                weight[:, h * HALF : (h + 1) * HALF],
+                MULT,
+            )
+
+        y00 = finish(0, 0)
+        gather(2, words2, 1, 2)
+        gather(3, words3, 1, 2)
+        y01 = finish(0, 1)
+        nc.vector.quantize_mx(out=u_codes[1][:].bitcast(FP8X4), scales=u_plane[1][:], in_=u_bf[1][:])
+        y10 = finish(1, 0)
+        y11 = finish(1, 1)
+        place(0, 0, y00)
+        place(0, 1, y01)
+        nc.sync.dma_start(out=out[0:P, :], in_=pages[0][:])
+        place(1, 0, y10)
+        place(1, 1, y11)
+        nc.sync.dma_start(out=out[P : 2 * P, :], in_=pages[1][:])

@@ -26,123 +26,127 @@ def tile_list_tabscat_d_none_kernel(tc, tab, w4_words, w4_scales, c, u, wgo, off
     nc = tc.nc
     with ExitStack() as ctx:
         keep = ctx.enter_context(tc.tile_pool(name="keep", bufs=1))
-        ring = ctx.enter_context(tc.tile_pool(name="ring", bufs=2))
         psum = ctx.enter_context(tc.psum_pool(name="psum", bufs=2))
 
         idx = keep.tile([P, S // 16], U16, name="idx")
         idx2 = keep.tile([P, S // 16], U16, name="idx2")
         win = keep.tile([P, T], U8, name="win", align_bytes=64)
-        w4 = keep.tile([P, PASSES, 2 * M], U8, name="w4", align_bytes=64)
-        rows = keep.tile([64, S + M], U8, name="rows", align_bytes=64)
-        planes = keep.tile([P, PASSES * (S + M)], U8, name="planes", align_bytes=64)
-        c_raw = keep.tile([P, PACK, S], F32, name="c_raw", tag="c_wgo", align_bytes=64)
-        u_raw = keep.tile([P, PACK, M], F32, name="u_raw", align_bytes=64)
+        w4_lo = keep.tile([P, 2, 2 * M], U8, name="w4_lo", align_bytes=64)
+        rows = keep.tile([P, S + M], U8, name="rows", align_bytes=64)
+        planes = [keep.tile([P, PASSES * 2 * HALF], U8, name="planes0", align_bytes=64)]
+        c_raw = keep.tile([P, PACK, S], F32, name="c_raw", tag="c_w4", align_bytes=64)
+        u_raw = keep.tile([P, PACK, M], F32, name="u_raw", tag="u_wgo", align_bytes=64)
+        early = keep.tile([P, 2 * T], U32, name="early", align_bytes=64)
         pages = [keep.tile([P, T], F32, name="page%d" % m, align_bytes=64) for m in range(2)]
 
-        nc.vector.memset(win[64:128, :].bitcast(I32), 0)
+        nc.vector.memset(win[0:32, :].bitcast(I32), 0)
+        nc.vector.memset(win[96:128, :].bitcast(I32), 0)
         for m in range(2):
             nc.vector.memset(pages[m][:], 0.0)
 
-        def load_words(a):
-            words = ring.tile([P, T], U32, name="words", align_bytes=64)
+        def load_words(a, window):
             nc.sync.dma_start(
-                out=words[:].bitcast(I32),
+                out=window.bitcast(I32),
                 in_=tab[a, 0 : 4 * P * T].rearrange("(p x) -> p x", p=P).bitcast(I32),
             )
-            return words
 
         nc.sync.dma_start(idx[:], offs)
-        nc.sync.dma_start(
-            out=win[0:64, :].bitcast(I32),
+        nc.scalar.dma_start(
+            out=win[32:96, :].bitcast(I32),
             in_=tab[:, 4 * P * T :].rearrange("a (q t) -> q a t", q=16).bitcast(I32),
         )
-        nc.scalar.dma_start(out=rows[:, S:].bitcast(I32), in_=w4_scales.rearrange("a q n -> q a n").bitcast(I32))
-        words0 = load_words(0)
-        nc.sync.dma_start(idx2[:], offs2)
-        words1 = load_words(1)
-        nc.sync.dma_start(out=w4[:].bitcast(I32), in_=w4_words.rearrange("a p n -> p a n").bitcast(I32))
+        nc.scalar.dma_start(out=rows[32:96, HALF : 3 * HALF].bitcast(I32), in_=w4_scales.rearrange("a q n -> q a n").bitcast(I32))
         nc.sync.dma_start(out=c_raw[:], in_=c.rearrange("(p j) w -> p j w", j=PACK))
+        load_words(0, early[:, :T])
+        nc.sync.dma_start(idx2[:], offs2)
         nc.sync.dma_start(out=u_raw[:], in_=u.rearrange("(p j) w -> p j w", j=PACK))
+        load_words(1, early[:, T:])
+        nc.sync.dma_start(out=w4_lo[:].bitcast(I32), in_=w4_words[0:2].rearrange("a p n -> p a n").bitcast(I32))
+
+        picked_scales = keep.tile([P, S], U8, name="picked_scales", tag="late", align_bytes=64)
+        nc.vector.tensor_copy(picked_scales[:], win[:].indirect(idx[:]))
+        nc.vector.tensor_copy(
+            rows[:].bitcast(I32).rearrange("p (x w) -> p x w", x=4)[:, 0:4:3, :],
+            picked_scales[:].bitcast(I32).rearrange("p (x w) -> p x w", x=2),
+        )
+
+        def spread(part):
+            for q in range(4):
+                nc.sync.dma_start(
+                    out=planes[part][32 * q : 32 * q + 4, :].rearrange("r (a n) -> r a n", a=PASSES).bitcast(I32),
+                    in_=rows[32 + 16 * q : 48 + 16 * q, part * 2 * HALF : (part + 1) * 2 * HALF].bitcast(I32),
+                )
+
+        spread(0)
+        late = keep.tile([P, 2 * T], U32, name="late", tag="late", align_bytes=64)
+        load_words(2, late[:, :T])
+        load_words(3, late[:, T:])
+        windows = [early[:, :T], early[:, T:], late[:, :T], late[:, T:]]
 
         picked = [keep.tile([P, S], U32, name="picked%d" % a, align_bytes=64) for a in range(PASSES)]
 
-        def gather(a, words, lo, hi):
+        def gather(a, lo, hi):
             nc.vector.tensor_copy(
-                picked[a][:, lo * HALF : hi * HALF], words[:].indirect(idx[:, lo * LIST_COLS : hi * LIST_COLS])
+                picked[a][:, lo * HALF : hi * HALF], windows[a].indirect(idx[:, lo * LIST_COLS : hi * LIST_COLS])
             )
 
-        picked_scales = keep.tile([P, S], U8, name="picked_scales", align_bytes=64)
-        nc.vector.tensor_copy(picked_scales[:], win[:].indirect(idx[:]))
-        nc.vector.tensor_copy(rows[:, :S].bitcast(I32), picked_scales[0:64, :].bitcast(I32))
-        for q in range(4):
-            nc.scalar.dma_start(
-                out=planes[32 * q : 32 * q + 4, :].rearrange("r (a n) -> r a n", a=PASSES).bitcast(I32),
-                in_=rows[16 * q : 16 * q + 16, :].bitcast(I32),
-            )
-        gather(0, words0, 0, 2)
-        words2 = load_words(2)
-        gather(1, words1, 0, 2)
-        words3 = load_words(3)
+        def interleave(raw, name):
+            grouped = keep.tile([P, PACK * 2 * HALF], BF16, name=name, tag=name, align_bytes=64)
+            for h, copy in enumerate((nc.vector.tensor_copy, nc.scalar.copy)):
+                copy(
+                    out=grouped[:, h * PACK * HALF : (h + 1) * PACK * HALF].rearrange(
+                        "p (c i t) -> p c t i", i=4, t=PACK
+                    ),
+                    in_=raw[:, :, h * HALF : (h + 1) * HALF].rearrange("p t (c i) -> p c t i", i=4),
+                )
+            return grouped
 
-        def views(raw, grouped):
-            return (
-                grouped.rearrange("p (c i t) -> p c t i", i=4, t=PACK),
-                raw.rearrange("p t (c i) -> p c t i", i=4),
-            )
+        def quantize(grouped, name):
+            codes = keep.tile([P, 2 * HALF], U32, name=name + "_codes", align_bytes=64)
+            plane = keep.tile([P, 2 * HALF], U8, name=name + "_plane", align_bytes=64)
+            nc.vector.quantize_mx(out=codes[:].bitcast(FP8X4), scales=plane[:], in_=grouped[:])
+            return codes, plane
 
-        c_bf = keep.tile([P, PACK * S], BF16, name="c_bf", align_bytes=64)
-        c_codes = keep.tile([P, S], U32, name="c_codes", align_bytes=64)
-        c_plane = keep.tile([P, S], U8, name="c_plane", align_bytes=64)
-        u_bf = [keep.tile([P, PACK * HALF], BF16, name="u_bf%d" % m, align_bytes=64) for m in range(2)]
-        u_codes = [keep.tile([P, HALF], U32, name="u_codes%d" % m, align_bytes=64) for m in range(2)]
-        u_plane = [keep.tile([P, HALF], U8, name="u_plane%d" % m, align_bytes=64) for m in range(2)]
-        acc = {}
+        c_bf = interleave(c_raw, "c_bf")
+        w4_hi = keep.tile([P, 2, 2 * M], U8, name="w4_hi", tag="c_w4", align_bytes=64)
+        nc.sync.dma_start(out=w4_hi[:].bitcast(I32), in_=w4_words[2:4].rearrange("a p n -> p a n").bitcast(I32))
+        gather(0, 0, 2)
+        c_codes, c_plane = quantize(c_bf, "c")
+        planes.append(keep.tile([P, PASSES * 2 * HALF], U8, name="planes1", tag="c_bf", align_bytes=64))
+        spread(1)
+        u_bf = interleave(u_raw, "u_bf")
+        weight = keep.tile([P, S], F32, name="weight", tag="u_wgo", align_bytes=64)
+        nc.sync.dma_start(out=weight[:], in_=wgo)
+        gather(1, 0, 2)
+        u_codes, u_plane = quantize(u_bf, "u")
 
-        def table_pass(a, m, h, start, stop):
-            at = a * (S + M)
+        def project(m, h):
+            acc = psum.tile([P, HALF], F32, name="acc")
+            rows_m = slice(m * HALF, (m + 1) * HALF)
+            cols_h = slice(h * HALF, (h + 1) * HALF)
             nc.tensor.matmul_mx(
-                out=acc[m, h][:],
-                lhsT=w4[:, a, 2 * m * HALF : 2 * (m + 1) * HALF].bitcast(FP4X4),
-                lhsT_scale=planes[:, at + S + m * HALF : at + S + (m + 1) * HALF],
-                rhs=picked[a][:, h * HALF : (h + 1) * HALF].bitcast(FP8X4),
-                rhs_scale=planes[:, at + h * HALF : at + (h + 1) * HALF],
-                start=start,
-                stop=stop,
-            )
-
-        def dense_pass(m, h):
-            nc.tensor.matmul_mx(
-                out=acc[m, h][:],
-                lhsT=u_codes[m][:].bitcast(FP8X4),
-                lhsT_scale=u_plane[m][:],
-                rhs=c_codes[:, h * HALF : (h + 1) * HALF].bitcast(FP8X4),
-                rhs_scale=c_plane[:, h * HALF : (h + 1) * HALF],
-                start=False,
+                out=acc[:],
+                lhsT=u_codes[:, rows_m].bitcast(FP8X4),
+                lhsT_scale=u_plane[:, rows_m],
+                rhs=c_codes[:, cols_h].bitcast(FP8X4),
+                rhs_scale=c_plane[:, cols_h],
+                start=True,
                 stop=False,
             )
-
-        dst, src = views(c_raw[:], c_bf[:])
-        nc.vector.tensor_copy(out=dst, in_=src)
-        weight = keep.tile([P, S], F32, name="weight", tag="c_wgo", align_bytes=64)
-        nc.sync.dma_start(out=weight[:], in_=wgo)
-        dst, src = views(u_raw[:, :, HALF:], u_bf[1][:])
-        nc.scalar.copy(out=dst, in_=src)
-        nc.vector.quantize_mx(out=c_codes[:].bitcast(FP8X4), scales=c_plane[:], in_=c_bf[:])
-        dst, src = views(u_raw[:, :, :HALF], u_bf[0][:])
-        nc.vector.tensor_copy(out=dst, in_=src)
-        gather(2, words2, 0, 1)
-        nc.vector.quantize_mx(out=u_codes[0][:].bitcast(FP8X4), scales=u_plane[0][:], in_=u_bf[0][:])
-        gather(3, words3, 0, 1)
-
-        def finish(m, h):
-            acc.setdefault((m, h), psum.tile([P, HALF], F32, name="acc"))
-            table_pass(0, m, h, True, False)
-            table_pass(1, m, h, False, False)
-            dense_pass(m, h)
-            table_pass(2, m, h, False, False)
-            table_pass(3, m, h, False, True)
+            for a in range(PASSES):
+                w_at = (2 * a + 1 - m) * HALF
+                t_at = (2 * a + h) * HALF
+                nc.tensor.matmul_mx(
+                    out=acc[:],
+                    lhsT=(w4_lo, w4_hi)[a // 2][:, a % 2, 2 * m * HALF : 2 * (m + 1) * HALF].bitcast(FP4X4),
+                    lhsT_scale=planes[m][:, w_at : w_at + HALF],
+                    rhs=picked[a][:, cols_h].bitcast(FP8X4),
+                    rhs_scale=planes[h][:, t_at : t_at + HALF],
+                    start=False,
+                    stop=(a == PASSES - 1),
+                )
             y = keep.tile([P, HALF], F32, name="y%d%d" % (m, h), align_bytes=64)
-            nc.scalar.copy(out=y[:], in_=acc[m, h][:])
+            nc.scalar.copy(out=y[:], in_=acc[:])
             return y
 
         def place(m, h, y):
@@ -153,16 +157,14 @@ def tile_list_tabscat_d_none_kernel(tc, tab, w4_words, w4_scales, c, u, wgo, off
                 MULT,
             )
 
-        y00 = finish(0, 0)
-        gather(2, words2, 1, 2)
-        gather(3, words3, 1, 2)
-        y01 = finish(0, 1)
-        nc.vector.quantize_mx(out=u_codes[1][:].bitcast(FP8X4), scales=u_plane[1][:], in_=u_bf[1][:])
-        y10 = finish(1, 0)
-        y11 = finish(1, 1)
-        place(0, 0, y00)
-        place(0, 1, y01)
-        nc.sync.dma_start(out=out[0:P, :], in_=pages[0][:])
-        place(1, 0, y10)
-        place(1, 1, y11)
-        nc.sync.dma_start(out=out[P : 2 * P, :], in_=pages[1][:])
+        ys = {}
+        gather(2, 0, 2)
+        for h in range(2):
+            gather(3, h, h + 1)
+            for m in range(2):
+                ys.setdefault((m, h), project(m, h))
+        for h in range(2):
+            for m in range(2):
+                place(m, h, ys[m, h])
+        for m in range(2):
+            nc.sync.dma_start(out=out[m * P : (m + 1) * P, :], in_=pages[m][:])

@@ -26,7 +26,7 @@ def tile_list_tabscat_d_none_kernel(tc, tab, w4_words, w4_scales, c, u, wgo, off
     nc = tc.nc
     with ExitStack() as ctx:
         keep = ctx.enter_context(tc.tile_pool(name="keep", bufs=1))
-        psum = ctx.enter_context(tc.psum_pool(name="psum", bufs=2))
+        psum = ctx.enter_context(tc.psum_pool(name="psum", bufs=4))
 
         idx = keep.tile([P, S // 16], U16, name="idx")
         idx2 = keep.tile([P, S // 16], U16, name="idx2")

from contextlib import ExitStack

import concourse.mybir as mybir

K, M, T, S, L = 2048, 256, 512, 256, 512
FLOPS = 2 * (K + L) * M * S

F32 = mybir.dt.float32
BF16 = mybir.dt.bfloat16
I32 = mybir.dt.int32
U32 = mybir.dt.uint32
U16 = mybir.dt.uint16
U8 = mybir.dt.uint8
FP8X4 = mybir.dt.float8_e4m3fn_x4
FP4X4 = mybir.dt.float4_e2m1fn_x4
MULT = mybir.AluOpType.mult

P = 128
PACK = 4
PASSES = K // (P * PACK)
HALF = 128
LIST_COLS = HALF // 16


def tile_list_tabscat_d_none_kernel(tc, tab, w4_words, w4_scales, c, u, wgo, offs, offs2, out):
    nc = tc.nc
    with ExitStack() as ctx:
        keep = ctx.enter_context(tc.tile_pool(name="keep", bufs=1))
        psum = ctx.enter_context(tc.psum_pool(name="psum", bufs=4))

        idx = keep.tile([P, S // 16], U16, name="idx")
        idx2 = keep.tile([P, S // 16], U16, name="idx2")
        win = keep.tile([P, T], U8, name="win", align_bytes=64)
        w4_lo = keep.tile([P, 2, 2 * M], U8, name="w4_lo", align_bytes=64)
        rows = keep.tile([P, S + M], U8, name="rows", align_bytes=64)
        planes = [keep.tile([P, PASSES * 2 * HALF], U8, name="planes0", align_bytes=64)]
        c_raw = keep.tile([P, PACK, S], F32, name="c_raw", tag="c_w4", align_bytes=64)
        u_raw = keep.tile([P, PACK, M], F32, name="u_raw", tag="u_wgo", align_bytes=64)
        early = keep.tile([P, 2 * T], U32, name="early", align_bytes=64)
        pages = [keep.tile([P, T], F32, name="page%d" % m, align_bytes=64) for m in range(2)]

        nc.vector.memset(win[0:32, :].bitcast(I32), 0)
        nc.vector.memset(win[96:128, :].bitcast(I32), 0)
        for m in range(2):
            nc.vector.memset(pages[m][:], 0.0)

        def load_words(a, window):
            nc.sync.dma_start(
                out=window.bitcast(I32),
                in_=tab[a, 0 : 4 * P * T].rearrange("(p x) -> p x", p=P).bitcast(I32),
            )

        nc.sync.dma_start(idx[:], offs)
        nc.scalar.dma_start(
            out=win[32:96, :].bitcast(I32),
            in_=tab[:, 4 * P * T :].rearrange("a (q t) -> q a t", q=16).bitcast(I32),
        )
        nc.scalar.dma_start(out=rows[32:96, HALF : 3 * HALF].bitcast(I32), in_=w4_scales.rearrange("a q n -> q a n").bitcast(I32))
        nc.sync.dma_start(out=c_raw[:], in_=c.rearrange("(p j) w -> p j w", j=PACK))
        load_words(0, early[:, :T])
        nc.sync.dma_start(idx2[:], offs2)
        nc.sync.dma_start(out=u_raw[:], in_=u.rearrange("(p j) w -> p j w", j=PACK))
        load_words(1, early[:, T:])
        nc.sync.dma_start(out=w4_lo[:].bitcast(I32), in_=w4_words[0:2].rearrange("a p n -> p a n").bitcast(I32))

        picked_scales = keep.tile([P, S], U8, name="picked_scales", tag="late", align_bytes=64)
        nc.vector.tensor_copy(picked_scales[:], win[:].indirect(idx[:]))
        nc.vector.tensor_copy(
            rows[:].bitcast(I32).rearrange("p (x w) -> p x w", x=4)[:, 0:4:3, :],
            picked_scales[:].bitcast(I32).rearrange("p (x w) -> p x w", x=2),
        )

        def spread(part):
            for q in range(4):
                nc.sync.dma_start(
                    out=planes[part][32 * q : 32 * q + 4, :].rearrange("r (a n) -> r a n", a=PASSES).bitcast(I32),
                    in_=rows[32 + 16 * q : 48 + 16 * q, part * 2 * HALF : (part + 1) * 2 * HALF].bitcast(I32),
                )

        spread(0)
        late = keep.tile([P, 2 * T], U32, name="late", tag="late", align_bytes=64)
        load_words(2, late[:, :T])
        load_words(3, late[:, T:])
        windows = [early[:, :T], early[:, T:], late[:, :T], late[:, T:]]

        picked = [keep.tile([P, S], U32, name="picked%d" % a, align_bytes=64) for a in range(PASSES)]

        def gather(a, lo, hi):
            nc.vector.tensor_copy(
                picked[a][:, lo * HALF : hi * HALF], windows[a].indirect(idx[:, lo * LIST_COLS : hi * LIST_COLS])
            )

        def interleave(raw, name):
            grouped = keep.tile([P, PACK * 2 * HALF], BF16, name=name, tag=name, align_bytes=64)
            for h, copy in enumerate((nc.vector.tensor_copy, nc.scalar.copy)):
                copy(
                    out=grouped[:, h * PACK * HALF : (h + 1) * PACK * HALF].rearrange(
                        "p (c i t) -> p c t i", i=4, t=PACK
                    ),
                    in_=raw[:, :, h * HALF : (h + 1) * HALF].rearrange("p t (c i) -> p c t i", i=4),
                )
            return grouped

        def quantize(grouped, name):
            codes = keep.tile([P, 2 * HALF], U32, name=name + "_codes", align_bytes=64)
            plane = keep.tile([P, 2 * HALF], U8, name=name + "_plane", align_bytes=64)
            nc.vector.quantize_mx(out=codes[:].bitcast(FP8X4), scales=plane[:], in_=grouped[:])
            return codes, plane

        c_bf = interleave(c_raw, "c_bf")
        w4_hi = keep.tile([P, 2, 2 * M], U8, name="w4_hi", tag="c_w4", align_bytes=64)
        nc.sync.dma_start(out=w4_hi[:].bitcast(I32), in_=w4_words[2:4].rearrange("a p n -> p a n").bitcast(I32))
        gather(0, 0, 2)
        c_codes, c_plane = quantize(c_bf, "c")
        planes.append(keep.tile([P, PASSES * 2 * HALF], U8, name="planes1", tag="c_bf", align_bytes=64))
        spread(1)
        u_bf = interleave(u_raw, "u_bf")
        weight = keep.tile([P, S], F32, name="weight", tag="u_wgo", align_bytes=64)
        nc.sync.dma_start(out=weight[:], in_=wgo)
        gather(1, 0, 2)
        u_codes, u_plane = quantize(u_bf, "u")

        def project(m, h):
            acc = psum.tile([P, HALF], F32, name="acc")
            rows_m = slice(m * HALF, (m + 1) * HALF)
            cols_h = slice(h * HALF, (h + 1) * HALF)
            nc.tensor.matmul_mx(
                out=acc[:],
                lhsT=u_codes[:, rows_m].bitcast(FP8X4),
                lhsT_scale=u_plane[:, rows_m],
                rhs=c_codes[:, cols_h].bitcast(FP8X4),
                rhs_scale=c_plane[:, cols_h],
                start=True,
                stop=False,
            )
            for a in range(PASSES):
                w_at = (2 * a + 1 - m) * HALF
                t_at = (2 * a + h) * HALF
                nc.tensor.matmul_mx(
                    out=acc[:],
                    lhsT=(w4_lo, w4_hi)[a // 2][:, a % 2, 2 * m * HALF : 2 * (m + 1) * HALF].bitcast(FP4X4),
                    lhsT_scale=planes[m][:, w_at : w_at + HALF],
                    rhs=picked[a][:, cols_h].bitcast(FP8X4),
                    rhs_scale=planes[h][:, t_at : t_at + HALF],
                    start=False,
                    stop=(a == PASSES - 1),
                )
            y = keep.tile([P, HALF], F32, name="y%d%d" % (m, h), align_bytes=64)
            nc.scalar.copy(out=y[:], in_=acc[:])
            return y

        def place(m, h, y):
            nc.vector.tensor_tensor(
                pages[m][:].indirect(idx2[:, h * LIST_COLS : (h + 1) * LIST_COLS]),
                y[:],
                weight[:, h * HALF : (h + 1) * HALF],
                MULT,
            )

        ys = {}
        gather(2, 0, 2)
        for h in range(2):
            gather(3, h, h + 1)
            for m in range(2):
                ys.setdefault((m, h), project(m, h))
        for h in range(2):
            for m in range(2):
                place(m, h, ys[m, h])
        for m in range(2):
            nc.sync.dma_start(out=out[m * P : (m + 1) * P, :], in_=pages[m][:])
